import numpy as np
import ml_dtypes


def mxq(x, axis, fmt="e4m3"):
    dtype, down = {"e4m3": (ml_dtypes.float8_e4m3fn, 7), "e5m2": (ml_dtypes.float8_e5m2, 14)}[fmt]
    v = np.moveaxis(np.asarray(x, np.float32).astype(ml_dtypes.bfloat16).astype(np.float64), axis, -1)
    blocks = v.reshape(v.shape[:-1] + (-1, 32))
    amax = np.abs(blocks).max(-1, keepdims=True)
    byte = np.maximum(np.where(amax > 0, np.frexp(amax)[1] - 1 + 127, 0) - down, 1)
    scale = np.exp2(byte - 127.0)
    codes = (blocks / scale).astype(np.float32).astype(dtype).astype(np.float64)
    return np.moveaxis((codes * scale).reshape(v.shape), -1, axis)


WIDE = False


def mx_kscale(k):
    if not WIDE:
        return np.ones(k)
    levels = np.array([10, -10, 5, -5, 0])
    if k % 512:
        return np.exp2(np.random.permutation(np.resize(levels, k // 32))).repeat(32)
    a = np.empty((k // 512, 16))
    for p in range(k // 512):
        a[p, :8] = np.random.permutation(np.resize(levels, 8))
        for g in range(8):
            far = levels[np.abs(levels - a[p, g]) >= 10]
            a[p, g + 8] = far[np.random.randint(len(far))]
    return np.exp2(a.ravel()).repeat(32)


def f64(x):
    return np.asarray(x).astype(np.float64)


def striped8(idx):
    return np.asarray(idx).reshape(8, -1, 16).transpose(0, 2, 1).reshape(128, -1).astype(np.uint16)


def unstriped8(offs):
    return offs.reshape(8, 16, -1).transpose(0, 2, 1).reshape(8, -1).astype(np.int64)


def pick8(x, idx, run):
    r = np.arange(len(x))
    return x[r[:, None], idx[r % (8 * run) // run]]


E2M1 = np.array([0.0, 0.5, 1.0, 1.5, 2.0, 3.0, 4.0, 6.0, -0.0, -0.5, -1.0, -1.5, -2.0, -3.0, -4.0, -6.0])


def pack_weight(w, fmt):
    k, n = w.shape
    w = f64(np.asarray(w, np.float32).astype(ml_dtypes.bfloat16)).reshape(k // 32, 32, n)
    amax = np.abs(w).max(1)
    if fmt == "e4m3":
        byte = np.frexp(amax)[1] - 1 + 127 - 7
    else:
        mant, ex = np.frexp(amax / 6.0)
        byte = np.where(mant > 0.5, ex, ex - 1) + 127
    byte = np.clip(np.where(amax > 0, byte, 1), 1, 254)
    scaled = (w * np.exp2(127.0 - byte)[:, None, :]).reshape(k, n).astype(np.float32)
    by_word = np.ascontiguousarray(scaled.reshape(k // 512, 128, 4, n).transpose(0, 1, 3, 2))
    if fmt == "e4m3":
        words = by_word.astype(ml_dtypes.float8_e4m3fn).view(np.uint8)
    else:
        c = by_word.astype(ml_dtypes.float4_e2m1fn).view(np.uint8) & 0xF
        words = (c[..., 0::2] | (c[..., 1::2] << 4)).reshape(k // 512, 128, 2 * n)
    return np.ascontiguousarray(words), np.ascontiguousarray(byte.astype(np.uint8).reshape(k // 512, 16, n))


def unpack_weight(words, scales, fmt):
    g, _, n = scales.shape
    words = np.ascontiguousarray(words).reshape(g, 128, n, -1)
    if fmt == "e4m3":
        vals = words.view(ml_dtypes.float8_e4m3fn).astype(np.float64)
    else:
        nib = np.empty((g, 128, n, 4), np.uint8)
        nib[..., 0::2] = words & 0xF
        nib[..., 1::2] = words >> 4
        vals = E2M1[nib]
    vals = vals * np.repeat(np.exp2(scales.astype(np.float64) - 127.0), 8, axis=1)[..., None]
    return vals.transpose(0, 1, 3, 2).reshape(g * 512, n)


D, K, T, U, Z, I, Q = 512, 512, 1024, 1024, 1024, 512, 128


def setup_inputs():
    n = np.random.standard_normal
    idx = np.stack([np.random.permutation(T)[:I] for _ in range(8)])
    idx2 = np.stack([np.random.permutation(U)[:I] for _ in range(8)])
    idx3 = np.stack([np.random.permutation(Z)[:I] for _ in range(8)])
    idx4 = np.stack([np.random.permutation(Z)[:I] for _ in range(8)])
    idx5 = np.stack([np.random.permutation(U)[:I] for _ in range(8)])
    idx6 = np.stack([np.random.permutation(T)[:I] for _ in range(8)])
    fd = mx_kscale(D)
    fk = mx_kscale(K)
    wqp = pack_weight(n((D, K)) * 1.0 / np.sqrt(D) * fd[:, None] * fk, "e4m3")
    keysp = pack_weight(n((K, T)) * 1.0 / np.sqrt(K) / fk[:, None], "e2m1")
    notesp = pack_weight(n((D, U)) * 1.0 / np.sqrt(D) * fd[:, None], "e4m3")
    return {
        "states": (n((D, Q)) * 0.95 / fd[:, None]).astype(np.float32),
        "wq_words": wqp[0],
        "wq_scales": wqp[1],
        "keys_words": keysp[0],
        "keys_scales": keysp[1],
        "notes_words": notesp[0],
        "notes_scales": notesp[1],
        "offs": striped8(idx),
        "offs2": striped8(idx2),
        "offs3": striped8(idx3),
        "offs4": striped8(idx4),
        "offs5": striped8(idx5),
        "offs6": striped8(idx6),
    }


def reference(states, wq_words, wq_scales, keys_words, keys_scales, notes_words, notes_scales, offs, offs2, offs3, offs4, offs5, offs6):
    idx = unstriped8(offs)
    idx2 = unstriped8(offs2)
    idx3 = unstriped8(offs3)
    idx4 = unstriped8(offs4)
    idx5 = unstriped8(offs5)
    idx6 = unstriped8(offs6)
    wqu = unpack_weight(wq_words, wq_scales, "e4m3")
    keysu = unpack_weight(keys_words, keys_scales, "e2m1")
    notesu = unpack_weight(notes_words, notes_scales, "e4m3")
    statesq = mxq(f64(states), 0, "e4m3")
    qv = wqu.T @ statesq
    qvq = mxq(qv, 0, "e4m3")
    a = qvq.T @ keysu
    b = statesq.T @ notesu
    f1 = np.zeros((Q, Z))
    f1[np.arange(Q)[:, None], idx3[np.arange(Q) % 128 // 16]] = pick8(a, idx, 16)
    f2 = np.zeros((Q, Z))
    f2[np.arange(Q)[:, None], idx4[np.arange(Q) % 128 // 16]] = pick8(b, idx2, 16)
    m1 = np.minimum(f1, f2)
    w = pick8(m1, idx3, 16) + pick8(m1, idx4, 16)
    v = w - pick8(b, idx5, 16)
    y = np.maximum(v, pick8(a, idx6, 16))
    return y

@@ -1,0 +1,166 @@
+from contextlib import ExitStack
+
+import concourse.mybir as mybir
+
+F32 = mybir.dt.float32
+BF16 = mybir.dt.bfloat16
+I32 = mybir.dt.int32
+U32 = mybir.dt.uint32
+U16 = mybir.dt.uint16
+U8 = mybir.dt.uint8
+FP8X4 = mybir.dt.float8_e4m3fn_x4
+FP4X4 = mybir.dt.float4_e2m1fn_x4
+ALU = mybir.AluOpType
+COPY = mybir.ActivationFunctionType.Copy
+
+P = 128
+D, K, T, U, Z, I, Q = 512, 512, 1024, 1024, 1024, 512, 128
+FLOPS = 2 * D * K * Q + 2 * K * Q * T + 2 * D * Q * U
+HALF = I // 2
+
+
+def cols(lo, hi):
+    return slice(lo // 16, hi // 16)
+
+
+def tile_attend_foldedback_madeside_kernel(tc, states, wq_words, wq_scales, keys_words, keys_scales,
+                                            notes_words, notes_scales, offs, offs2, offs3, offs4, offs5,
+                                            offs6, out):
+    nc = tc.nc
+    with ExitStack() as ctx:
+        keep = ctx.enter_context(tc.tile_pool(name="keep", bufs=1))
+        psum = ctx.enter_context(tc.psum_pool(name="psum", bufs=1))
+
+        def scale_tile(name, n):
+            t = keep.tile([P, 2 * n], U8, name=name, align_bytes=64)
+            nc.vector.memset(t[0:64, :].bitcast(I32), 0)
+            return t
+
+        def load_scales(queue, t, src, n):
+            rows = src[0].bitcast(I32).rearrange("(h g r) n -> g r h n", h=2, g=2)
+            for g in range(2):
+                queue.dma_start(t[32 * g:32 * g + 4, :].bitcast(I32).rearrange("r (h n) -> r h n", h=2), rows[g])
+
+        def lift_scales(t, n):
+            nc.vector.tensor_copy(t[64:128, 0:n].bitcast(I32), t[0:64, n:2 * n].bitcast(I32))
+
+        def load_list(name, src):
+            t = keep.tile([P, I // 16], U16, name=name)
+            nc.sync.dma_start(t[:], src)
+            return t
+
+        ns = scale_tile("ns", U)
+        ws = scale_tile("ws", K)
+        ks = scale_tile("ks", T)
+
+        raw = keep.tile([P, 4, Q], F32, name="raw")
+        nc.sync.dma_start(raw[:], states.rearrange("(p j) q -> p j q", j=4))
+        load_scales(nc.scalar, ns, notes_scales, U)
+        nw_src = notes_words[0].rearrange("p n t -> p (n t)").bitcast(I32)
+        nw = [keep.tile([P, 512], U32, name="nw%d" % h, align_bytes=64) for h in range(2)]
+        nc.sync.dma_start(nw[0][:].bitcast(I32), nw_src[:, 0:512])
+        load_scales(nc.scalar, ws, wq_scales, K)
+        ww = keep.tile([P, K], U32, name="ww", align_bytes=64)
+        nc.sync.dma_start(ww[:].bitcast(I32), wq_words[0].rearrange("p n t -> p (n t)").bitcast(I32))
+        nc.sync.dma_start(nw[1][:].bitcast(I32), nw_src[:, 512:1024])
+        o2 = load_list("o2", offs2)
+        o4 = load_list("o4", offs4)
+        kw = keep.tile([P, 2 * T], U8, name="kw", align_bytes=64)
+        nc.sync.dma_start(kw[:].bitcast(I32), keys_words[0].bitcast(I32))
+        load_scales(nc.sync, ks, keys_scales, T)
+        o1 = load_list("o1", offs)
+        o3 = load_list("o3", offs3)
+        o5 = load_list("o5", offs5)
+        o6 = load_list("o6", offs6)
+
+        f2 = keep.tile([P, Z], F32, name="f2")
+        f1 = keep.tile([P, Z], F32, name="f1")
+        nc.vector.memset(f2[:], 0.0)
+        nc.vector.memset(f1[:], 0.0)
+
+        sb = keep.tile([P, Q, 4], BF16, name="sb", align_bytes=64)
+        nc.vector.tensor_copy(sb[:].rearrange("p (c i) t -> p c t i", i=4),
+                              raw[:].rearrange("p t (c i) -> p c t i", i=4))
+        lift_scales(ns, U)
+        sq = keep.tile([P, Q], U32, name="sq", align_bytes=64)
+        ss = keep.tile([P, Q], U8, name="ss", align_bytes=64)
+        nc.vector.quantize_mx(out=sq[:].bitcast(FP8X4), scales=ss[:], in_=sb[:].rearrange("p q t -> p (q t)"))
+
+        b = keep.tile([P, U], F32, name="b")
+        pieces = ((0, 512, nc.scalar), (512, 768, nc.vector), (768, 1024, nc.scalar))
+        b_ps = []
+        for n, (lo, hi, eng) in enumerate(pieces):
+            ps = psum.tile([P, hi - lo], F32, name="b_ps%d" % n)
+            nc.tensor.matmul_mx(out=ps[:], lhsT=sq[:].bitcast(FP8X4), lhsT_scale=ss[:],
+                                rhs=nw[lo // 512][:, lo % 512:lo % 512 + hi - lo].bitcast(FP8X4),
+                                rhs_scale=ns[:, lo:hi], start=True, stop=True)
+            b_ps.append(ps)
+
+        lift_scales(ws, K)
+        wsd = keep.tile([P, K], U8, name="wsd", align_bytes=64)
+        nc.vector.tensor_copy(wsd[:].rearrange("p (t c i) -> p c t i", t=4, i=16),
+                              ws[:, 0:K].rearrange("p (c i t) -> p c t i", t=4, i=16))
+
+        wwd = keep.tile([P, K], U32, name="wwd", tag="wwd", align_bytes=64)
+        nc.vector.tensor_copy(wwd[:].bitcast(I32).rearrange("p (t c i) -> p c t i", t=4, i=4),
+                              ww[:].bitcast(I32).rearrange("p (c i t) -> p c t i", t=4, i=4))
+
+        nc.scalar.activation(b[:, 0:512], b_ps[0][:], COPY)
+        nc.vector.tensor_copy(b[:, 512:768], b_ps[1][:])
+        nc.scalar.activation(b[:, 768:1024], b_ps[2][:], COPY)
+
+        qv_ps = psum.tile([P, 4, Q], F32, name="qv_ps")
+        for t in range(4):
+            nc.tensor.matmul_mx(out=qv_ps[:, t, :], lhsT=wwd[:, P * t:P * (t + 1)].bitcast(FP8X4),
+                                lhsT_scale=wsd[:, P * t:P * (t + 1)], rhs=sq[:].bitcast(FP8X4),
+                                rhs_scale=ss[:], start=True, stop=True)
+
+        gb = keep.tile([P, I], F32, name="gb", tag="wwd", align_bytes=64)
+        nc.vector.tensor_copy(gb[:, 0:HALF], b[:].indirect(o2[:, cols(0, HALF)]))
+        lift_scales(ks, T)
+
+        qb = keep.tile([P, Q, 4], BF16, name="qb", align_bytes=64)
+        nc.scalar.activation(qb[:], qv_ps[:].rearrange("p t q -> p q t"), COPY)
+        nc.scalar.activation(gb[:, HALF:I], b[:].indirect(o2[:, cols(HALF, I)]), COPY)
+
+        nc.vector.tensor_copy(f2[:].indirect(o4[:, cols(0, 128)]), gb[:, 0:128])
+        qq = keep.tile([P, Q], U32, name="qq", align_bytes=64)
+        qs = keep.tile([P, Q], U8, name="qs", align_bytes=64)
+        nc.vector.quantize_mx(out=qq[:].bitcast(FP8X4), scales=qs[:], in_=qb[:].rearrange("p q t -> p (q t)"))
+        nc.vector.tensor_copy(f2[:].indirect(o4[:, cols(128, I)]), gb[:, 128:I])
+
+        a = keep.tile([P, T], F32, name="a")
+        for h in range(4):
+            ps = psum.tile([P, 256], F32, name="a_ps%d" % h)
+            nc.tensor.matmul_mx(out=ps[:], lhsT=qq[:].bitcast(FP8X4), lhsT_scale=qs[:],
+                                rhs=kw[:, 512 * h:512 * (h + 1)].bitcast(FP4X4),
+                                rhs_scale=ks[:, 256 * h:256 * (h + 1)], start=True, stop=True)
+            nc.scalar.activation(a[:, 256 * h:256 * (h + 1)], ps[:], COPY)
+
+        ga = [keep.tile([P, HALF], F32, name="ga%d" % h, tag="ga%d" % h) for h in range(2)]
+        for h in range(2):
+            nc.scalar.activation(ga[h][:], a[:].indirect(o1[:, cols(HALF * h, HALF * (h + 1))]), COPY)
+        for h in range(2):
+            nc.vector.tensor_copy(f1[:].indirect(o3[:, cols(HALF * h, HALF * (h + 1))]), ga[h][:])
+        a6 = keep.tile([P, I], F32, name="a6")
+        nc.scalar.activation(a6[:], a[:].indirect(o6[:]), COPY)
+        b5 = keep.tile([P, I], F32, name="b5", tag="ga0")
+        nc.scalar.activation(b5[:], b[:].indirect(o5[:]), COPY)
+
+        m1 = keep.tile([P, Z], F32, name="m1")
+        nc.vector.tensor_tensor(m1[:], f1[:], f2[:], ALU.min)
+
+        g3 = [keep.tile([P, HALF], F32, name="g3%d" % h) for h in range(2)]
+        t4 = [keep.tile([P, HALF], F32, name="t4%d" % h) for h in range(2)]
+        v = [keep.tile([P, HALF], F32, name="v%d" % h) for h in range(2)]
+        y = [keep.tile([P, HALF], F32, name="y%d" % h) for h in range(2)]
+        for h in range(2):
+            s = slice(HALF * h, HALF * (h + 1))
+            nc.scalar.activation(g3[h][:], m1[:].indirect(o3[:, cols(s.start, s.stop)]), COPY)
+            nc.vector.tensor_tensor(t4[h][:], m1[:].indirect(o4[:, cols(s.start, s.stop)]), b5[:, s], ALU.subtract)
+        for h in range(2):
+            nc.vector.tensor_tensor(v[h][:], t4[h][:], g3[h][:], ALU.add)
+        for h in range(2):
+            s = slice(HALF * h, HALF * (h + 1))
+            nc.vector.tensor_tensor(y[h][:], v[h][:], a6[:, s], ALU.max)
+            nc.sync.dma_start(out[:, s], y[h][:])

@@ -33,16 +33,18 @@ def tile_attend_foldedback_madeside_kernel(tc, states, wq_words, wq_scales, keys
 
         def scale_tile(name, n):
             t = keep.tile([P, 2 * n], U8, name=name, align_bytes=64)
-            nc.vector.memset(t[0:64, :].bitcast(I32), 0)
+            nc.vector.memset(t[:, 0:n].bitcast(I32), 0)
             return t
 
         def load_scales(queue, t, src, n):
-            rows = src[0].bitcast(I32).rearrange("(h g r) n -> g r h n", h=2, g=2)
+            rows = src[0].bitcast(I32).rearrange("(g h r) n -> g r h n", h=2, g=2)
             for g in range(2):
-                queue.dma_start(t[32 * g:32 * g + 4, :].bitcast(I32).rearrange("r (h n) -> r h n", h=2), rows[g])
+                queue.dma_start(t[64 * g:64 * g + 4, :].bitcast(I32).rearrange("r (h n) -> r h n", h=2), rows[g])
 
         def lift_scales(t, n):
-            nc.vector.tensor_copy(t[64:128, 0:n].bitcast(I32), t[0:64, n:2 * n].bitcast(I32))
+            for g in range(2):
+                nc.vector.tensor_copy(t[64 * g + 32:64 * g + 36, 0:n].bitcast(I32),
+                                      t[64 * g:64 * g + 4, n:2 * n].bitcast(I32))
 
         def load_list(name, src):
             t = keep.tile([P, I // 16], U16, name=name)
@@ -51,32 +53,32 @@ def tile_attend_foldedback_madeside_kernel(tc, states, wq_words, wq_scales, keys
 
         ns = scale_tile("ns", U)
         ws = scale_tile("ws", K)
-        ks = scale_tile("ks", T)
+        ks = keep.tile([P, T], U8, name="ks", align_bytes=64)
+        nc.vector.memset(ks[:].bitcast(I32), 0)
 
         raw = keep.tile([P, 4, Q], F32, name="raw")
         nc.sync.dma_start(raw[:], states.rearrange("(p j) q -> p j q", j=4))
-        load_scales(nc.scalar, ns, notes_scales, U)
+        load_scales(nc.sync, ns, notes_scales, U)
         nw_src = notes_words[0].rearrange("p n t -> p (n t)").bitcast(I32)
         nw = [keep.tile([P, 512], U32, name="nw%d" % h, align_bytes=64) for h in range(2)]
         nc.sync.dma_start(nw[0][:].bitcast(I32), nw_src[:, 0:512])
         load_scales(nc.scalar, ws, wq_scales, K)
-        ww = keep.tile([P, K], U32, name="ww", align_bytes=64)
+        ww = keep.tile([P, K], U32, name="ww", tag="ww", align_bytes=64)
         nc.sync.dma_start(ww[:].bitcast(I32), wq_words[0].rearrange("p n t -> p (n t)").bitcast(I32))
-        nc.sync.dma_start(nw[1][:].bitcast(I32), nw_src[:, 512:1024])
         o2 = load_list("o2", offs2)
+        nc.sync.dma_start(nw[1][:].bitcast(I32), nw_src[:, 512:1024])
         o4 = load_list("o4", offs4)
         kw = keep.tile([P, 2 * T], U8, name="kw", align_bytes=64)
         nc.sync.dma_start(kw[:].bitcast(I32), keys_words[0].bitcast(I32))
-        load_scales(nc.sync, ks, keys_scales, T)
+        for g in range(4):
+            nc.sync.dma_start(ks[32 * g:32 * g + 4, :].bitcast(I32), keys_scales[0].bitcast(I32)[4 * g:4 * g + 4, :])
         o1 = load_list("o1", offs)
         o3 = load_list("o3", offs3)
         o5 = load_list("o5", offs5)
         o6 = load_list("o6", offs6)
 
         f2 = keep.tile([P, Z], F32, name="f2")
-        f1 = keep.tile([P, Z], F32, name="f1")
         nc.vector.memset(f2[:], 0.0)
-        nc.vector.memset(f1[:], 0.0)
 
         sb = keep.tile([P, Q, 4], BF16, name="sb", align_bytes=64)
         nc.vector.tensor_copy(sb[:].rearrange("p (c i) t -> p c t i", i=4),
@@ -87,64 +89,61 @@ def tile_attend_foldedback_madeside_kernel(tc, states, wq_words, wq_scales, keys
         nc.vector.quantize_mx(out=sq[:].bitcast(FP8X4), scales=ss[:], in_=sb[:].rearrange("p q t -> p (q t)"))
 
         b = keep.tile([P, U], F32, name="b")
-        pieces = ((0, 512, nc.scalar), (512, 768, nc.vector), (768, 1024, nc.scalar))
-        b_ps = []
-        for n, (lo, hi, eng) in enumerate(pieces):
-            ps = psum.tile([P, hi - lo], F32, name="b_ps%d" % n)
+
+        def b_pass(lo, hi):
+            ps = psum.tile([P, hi - lo], F32, name="b_ps%d" % lo, tag="bank%d" % lo)
             nc.tensor.matmul_mx(out=ps[:], lhsT=sq[:].bitcast(FP8X4), lhsT_scale=ss[:],
                                 rhs=nw[lo // 512][:, lo % 512:lo % 512 + hi - lo].bitcast(FP8X4),
                                 rhs_scale=ns[:, lo:hi], start=True, stop=True)
-            b_ps.append(ps)
+            return ps
+
+        nc.scalar.activation(b[:, 0:512], b_pass(0, 512)[:], COPY)
 
         lift_scales(ws, K)
         wsd = keep.tile([P, K], U8, name="wsd", align_bytes=64)
         nc.vector.tensor_copy(wsd[:].rearrange("p (t c i) -> p c t i", t=4, i=16),
                               ws[:, 0:K].rearrange("p (c i t) -> p c t i", t=4, i=16))
-
         wwd = keep.tile([P, K], U32, name="wwd", tag="wwd", align_bytes=64)
         nc.vector.tensor_copy(wwd[:].bitcast(I32).rearrange("p (t c i) -> p c t i", t=4, i=4),
                               ww[:].bitcast(I32).rearrange("p (c i t) -> p c t i", t=4, i=4))
-
-        nc.scalar.activation(b[:, 0:512], b_ps[0][:], COPY)
-        nc.vector.tensor_copy(b[:, 512:768], b_ps[1][:])
-        nc.scalar.activation(b[:, 768:1024], b_ps[2][:], COPY)
+        f1 = keep.tile([P, Z], F32, name="f1", tag="ww", align_bytes=64)
+        nc.gpsimd.memset(f1[:], 0.0)
 
         qv_ps = psum.tile([P, 4, Q], F32, name="qv_ps")
         for t in range(4):
             nc.tensor.matmul_mx(out=qv_ps[:, t, :], lhsT=wwd[:, P * t:P * (t + 1)].bitcast(FP8X4),
                                 lhsT_scale=wsd[:, P * t:P * (t + 1)], rhs=sq[:].bitcast(FP8X4),
                                 rhs_scale=ss[:], start=True, stop=True)
-
-        gb = keep.tile([P, I], F32, name="gb", tag="wwd", align_bytes=64)
-        nc.vector.tensor_copy(gb[:, 0:HALF], b[:].indirect(o2[:, cols(0, HALF)]))
-        lift_scales(ks, T)
-
         qb = keep.tile([P, Q, 4], BF16, name="qb", align_bytes=64)
         nc.scalar.activation(qb[:], qv_ps[:].rearrange("p t q -> p q t"), COPY)
-        nc.scalar.activation(gb[:, HALF:I], b[:].indirect(o2[:, cols(HALF, I)]), COPY)
 
-        nc.vector.tensor_copy(f2[:].indirect(o4[:, cols(0, 128)]), gb[:, 0:128])
+        nc.vector.tensor_copy(b[:, 512:768], b_pass(512, 768)[:])
+        nc.vector.tensor_copy(b[:, 768:896], b_pass(768, 896)[:])
+        nc.scalar.activation(b[:, 896:1024], b_pass(896, 1024)[:], COPY)
+
         qq = keep.tile([P, Q], U32, name="qq", align_bytes=64)
         qs = keep.tile([P, Q], U8, name="qs", align_bytes=64)
         nc.vector.quantize_mx(out=qq[:].bitcast(FP8X4), scales=qs[:], in_=qb[:].rearrange("p q t -> p (q t)"))
-        nc.vector.tensor_copy(f2[:].indirect(o4[:, cols(128, I)]), gb[:, 128:I])
 
-        a = keep.tile([P, T], F32, name="a")
+        gb = keep.tile([P, I], F32, name="gb", tag="wwd", align_bytes=64)
+        nc.vector.tensor_copy(gb[:, 0:HALF], b[:].indirect(o2[:, cols(0, HALF)]))
+        nc.scalar.activation(gb[:, HALF:I], b[:].indirect(o2[:, cols(HALF, I)]), COPY)
+        nc.vector.tensor_copy(f2[:].indirect(o4[:]), gb[:])
+
+        a = keep.tile([P, T], F32, name="a", tag="a")
         for h in range(4):
-            ps = psum.tile([P, 256], F32, name="a_ps%d" % h)
+            ps = psum.tile([P, 256], F32, name="a_ps%d" % h, tag="bank%d" % h)
             nc.tensor.matmul_mx(out=ps[:], lhsT=qq[:].bitcast(FP8X4), lhsT_scale=qs[:],
                                 rhs=kw[:, 512 * h:512 * (h + 1)].bitcast(FP4X4),
                                 rhs_scale=ks[:, 256 * h:256 * (h + 1)], start=True, stop=True)
             nc.scalar.activation(a[:, 256 * h:256 * (h + 1)], ps[:], COPY)
 
-        ga = [keep.tile([P, HALF], F32, name="ga%d" % h, tag="ga%d" % h) for h in range(2)]
-        for h in range(2):
-            nc.scalar.activation(ga[h][:], a[:].indirect(o1[:, cols(HALF * h, HALF * (h + 1))]), COPY)
-        for h in range(2):
-            nc.vector.tensor_copy(f1[:].indirect(o3[:, cols(HALF * h, HALF * (h + 1))]), ga[h][:])
+        ga = keep.tile([P, I], F32, name="ga")
+        nc.scalar.activation(ga[:], a[:].indirect(o1[:]), COPY)
+        nc.vector.tensor_copy(f1[:].indirect(o3[:]), ga[:])
         a6 = keep.tile([P, I], F32, name="a6")
         nc.scalar.activation(a6[:], a[:].indirect(o6[:]), COPY)
-        b5 = keep.tile([P, I], F32, name="b5", tag="ga0")
+        b5 = keep.tile([P, I], F32, name="b5", tag="a")
         nc.scalar.activation(b5[:], b[:].indirect(o5[:]), COPY)
 
         m1 = keep.tile([P, Z], F32, name="m1")

@@ -101,19 +101,20 @@ def tile_attend_foldedback_madeside_kernel(tc, states, wq_words, wq_scales, keys
 
         lift_scales(ws, K)
         wsd = keep.tile([P, K], U8, name="wsd", align_bytes=64)
-        nc.vector.tensor_copy(wsd[:].rearrange("p (t c i) -> p c t i", t=4, i=16),
-                              ws[:, 0:K].rearrange("p (c i t) -> p c t i", t=4, i=16))
         wwd = keep.tile([P, K], U32, name="wwd", tag="wwd", align_bytes=64)
-        nc.vector.tensor_copy(wwd[:].bitcast(I32).rearrange("p (t c i) -> p c t i", t=4, i=4),
-                              ww[:].bitcast(I32).rearrange("p (c i t) -> p c t i", t=4, i=4))
+        qv_ps = psum.tile([P, 4, Q], F32, name="qv_ps")
+        for u in range(2):
+            pair = slice(2 * u, 2 * u + 2)
+            nc.vector.tensor_copy(wsd[:].rearrange("p (t c i) -> p c t i", t=4, i=16)[:, :, pair, :],
+                                  ws[:, 0:K].rearrange("p (c i t) -> p c t i", t=4, i=16)[:, :, pair, :])
+            nc.vector.tensor_copy(wwd[:].bitcast(I32).rearrange("p (t c i) -> p c t i", t=4, i=4)[:, :, pair, :],
+                                  ww[:].bitcast(I32).rearrange("p (c i t) -> p c t i", t=4, i=4)[:, :, pair, :])
+            for t in range(2 * u, 2 * u + 2):
+                nc.tensor.matmul_mx(out=qv_ps[:, t, :], lhsT=wwd[:, P * t:P * (t + 1)].bitcast(FP8X4),
+                                    lhsT_scale=wsd[:, P * t:P * (t + 1)], rhs=sq[:].bitcast(FP8X4),
+                                    rhs_scale=ss[:], start=True, stop=True)
         f1 = keep.tile([P, Z], F32, name="f1", tag="ww", align_bytes=64)
         nc.gpsimd.memset(f1[:], 0.0)
-
-        qv_ps = psum.tile([P, 4, Q], F32, name="qv_ps")
-        for t in range(4):
-            nc.tensor.matmul_mx(out=qv_ps[:, t, :], lhsT=wwd[:, P * t:P * (t + 1)].bitcast(FP8X4),
-                                lhsT_scale=wsd[:, P * t:P * (t + 1)], rhs=sq[:].bitcast(FP8X4),
-                                rhs_scale=ss[:], start=True, stop=True)
         qb = keep.tile([P, Q, 4], BF16, name="qb", align_bytes=64)
         nc.scalar.activation(qb[:], qv_ps[:].rearrange("p t q -> p q t"), COPY)
 

from contextlib import ExitStack

import concourse.mybir as mybir

F32 = mybir.dt.float32
BF16 = mybir.dt.bfloat16
I32 = mybir.dt.int32
U32 = mybir.dt.uint32
U16 = mybir.dt.uint16
U8 = mybir.dt.uint8
FP8X4 = mybir.dt.float8_e4m3fn_x4
FP4X4 = mybir.dt.float4_e2m1fn_x4
ALU = mybir.AluOpType
COPY = mybir.ActivationFunctionType.Copy

P = 128
D, K, T, U, Z, I, Q = 512, 512, 1024, 1024, 1024, 512, 128
FLOPS = 2 * D * K * Q + 2 * K * Q * T + 2 * D * Q * U
HALF = I // 2


def cols(lo, hi):
    return slice(lo // 16, hi // 16)


def tile_attend_foldedback_madeside_kernel(tc, states, wq_words, wq_scales, keys_words, keys_scales,
                                            notes_words, notes_scales, offs, offs2, offs3, offs4, offs5,
                                            offs6, out):
    nc = tc.nc
    with ExitStack() as ctx:
        keep = ctx.enter_context(tc.tile_pool(name="keep", bufs=1))
        psum = ctx.enter_context(tc.psum_pool(name="psum", bufs=1))

        def scale_tile(name, n):
            t = keep.tile([P, 2 * n], U8, name=name, align_bytes=64)
            nc.vector.memset(t[:, 0:n].bitcast(I32), 0)
            return t

        def load_scales(queue, t, src, n):
            rows = src[0].bitcast(I32).rearrange("(g h r) n -> g r h n", h=2, g=2)
            for g in range(2):
                queue.dma_start(t[64 * g:64 * g + 4, :].bitcast(I32).rearrange("r (h n) -> r h n", h=2), rows[g])

        def lift_scales(t, n):
            for g in range(2):
                nc.vector.tensor_copy(t[64 * g + 32:64 * g + 36, 0:n].bitcast(I32),
                                      t[64 * g:64 * g + 4, n:2 * n].bitcast(I32))

        def load_list(name, src):
            t = keep.tile([P, I // 16], U16, name=name)
            nc.sync.dma_start(t[:], src)
            return t

        ns = scale_tile("ns", U)
        ws = scale_tile("ws", K)
        ks = keep.tile([P, T], U8, name="ks", align_bytes=64)
        nc.vector.memset(ks[:].bitcast(I32), 0)

        raw = keep.tile([P, 4, Q], F32, name="raw")
        nc.sync.dma_start(raw[:], states.rearrange("(p j) q -> p j q", j=4))
        load_scales(nc.sync, ns, notes_scales, U)
        nw_src = notes_words[0].rearrange("p n t -> p (n t)").bitcast(I32)
        nw = [keep.tile([P, 512], U32, name="nw%d" % h, align_bytes=64) for h in range(2)]
        nc.sync.dma_start(nw[0][:].bitcast(I32), nw_src[:, 0:512])
        load_scales(nc.scalar, ws, wq_scales, K)
        ww = keep.tile([P, K], U32, name="ww", tag="ww", align_bytes=64)
        nc.sync.dma_start(ww[:].bitcast(I32), wq_words[0].rearrange("p n t -> p (n t)").bitcast(I32))
        o2 = load_list("o2", offs2)
        nc.sync.dma_start(nw[1][:].bitcast(I32), nw_src[:, 512:1024])
        o4 = load_list("o4", offs4)
        kw = keep.tile([P, 2 * T], U8, name="kw", align_bytes=64)
        nc.sync.dma_start(kw[:].bitcast(I32), keys_words[0].bitcast(I32))
        for g in range(4):
            nc.sync.dma_start(ks[32 * g:32 * g + 4, :].bitcast(I32), keys_scales[0].bitcast(I32)[4 * g:4 * g + 4, :])
        o1 = load_list("o1", offs)
        o3 = load_list("o3", offs3)
        o5 = load_list("o5", offs5)
        o6 = load_list("o6", offs6)

        f2 = keep.tile([P, Z], F32, name="f2")
        nc.vector.memset(f2[:], 0.0)

        sb = keep.tile([P, Q, 4], BF16, name="sb", align_bytes=64)
        nc.vector.tensor_copy(sb[:].rearrange("p (c i) t -> p c t i", i=4),
                              raw[:].rearrange("p t (c i) -> p c t i", i=4))
        lift_scales(ns, U)
        sq = keep.tile([P, Q], U32, name="sq", align_bytes=64)
        ss = keep.tile([P, Q], U8, name="ss", align_bytes=64)
        nc.vector.quantize_mx(out=sq[:].bitcast(FP8X4), scales=ss[:], in_=sb[:].rearrange("p q t -> p (q t)"))

        b = keep.tile([P, U], F32, name="b")

        def b_pass(lo, hi):
            ps = psum.tile([P, hi - lo], F32, name="b_ps%d" % lo, tag="bank%d" % lo)
            nc.tensor.matmul_mx(out=ps[:], lhsT=sq[:].bitcast(FP8X4), lhsT_scale=ss[:],
                                rhs=nw[lo // 512][:, lo % 512:lo % 512 + hi - lo].bitcast(FP8X4),
                                rhs_scale=ns[:, lo:hi], start=True, stop=True)
            return ps

        nc.scalar.activation(b[:, 0:512], b_pass(0, 512)[:], COPY)

        lift_scales(ws, K)
        wsd = keep.tile([P, K], U8, name="wsd", align_bytes=64)
        wwd = keep.tile([P, K], U32, name="wwd", tag="wwd", align_bytes=64)
        qv_ps = psum.tile([P, 4, Q], F32, name="qv_ps")
        for u in range(2):
            pair = slice(2 * u, 2 * u + 2)
            nc.vector.tensor_copy(wsd[:].rearrange("p (t c i) -> p c t i", t=4, i=16)[:, :, pair, :],
                                  ws[:, 0:K].rearrange("p (c i t) -> p c t i", t=4, i=16)[:, :, pair, :])
            nc.vector.tensor_copy(wwd[:].bitcast(I32).rearrange("p (t c i) -> p c t i", t=4, i=4)[:, :, pair, :],
                                  ww[:].bitcast(I32).rearrange("p (c i t) -> p c t i", t=4, i=4)[:, :, pair, :])
            for t in range(2 * u, 2 * u + 2):
                nc.tensor.matmul_mx(out=qv_ps[:, t, :], lhsT=wwd[:, P * t:P * (t + 1)].bitcast(FP8X4),
                                    lhsT_scale=wsd[:, P * t:P * (t + 1)], rhs=sq[:].bitcast(FP8X4),
                                    rhs_scale=ss[:], start=True, stop=True)
        f1 = keep.tile([P, Z], F32, name="f1", tag="ww", align_bytes=64)
        nc.gpsimd.memset(f1[:], 0.0)
        qb = keep.tile([P, Q, 4], BF16, name="qb", align_bytes=64)
        nc.scalar.activation(qb[:], qv_ps[:].rearrange("p t q -> p q t"), COPY)

        nc.vector.tensor_copy(b[:, 512:768], b_pass(512, 768)[:])
        nc.vector.tensor_copy(b[:, 768:896], b_pass(768, 896)[:])
        nc.scalar.activation(b[:, 896:1024], b_pass(896, 1024)[:], COPY)

        qq = keep.tile([P, Q], U32, name="qq", align_bytes=64)
        qs = keep.tile([P, Q], U8, name="qs", align_bytes=64)
        nc.vector.quantize_mx(out=qq[:].bitcast(FP8X4), scales=qs[:], in_=qb[:].rearrange("p q t -> p (q t)"))

        gb = keep.tile([P, I], F32, name="gb", tag="wwd", align_bytes=64)
        nc.vector.tensor_copy(gb[:, 0:HALF], b[:].indirect(o2[:, cols(0, HALF)]))
        nc.scalar.activation(gb[:, HALF:I], b[:].indirect(o2[:, cols(HALF, I)]), COPY)
        nc.vector.tensor_copy(f2[:].indirect(o4[:]), gb[:])

        a = keep.tile([P, T], F32, name="a", tag="a")
        for h in range(4):
            ps = psum.tile([P, 256], F32, name="a_ps%d" % h, tag="bank%d" % h)
            nc.tensor.matmul_mx(out=ps[:], lhsT=qq[:].bitcast(FP8X4), lhsT_scale=qs[:],
                                rhs=kw[:, 512 * h:512 * (h + 1)].bitcast(FP4X4),
                                rhs_scale=ks[:, 256 * h:256 * (h + 1)], start=True, stop=True)
            nc.scalar.activation(a[:, 256 * h:256 * (h + 1)], ps[:], COPY)

        ga = keep.tile([P, I], F32, name="ga")
        nc.scalar.activation(ga[:], a[:].indirect(o1[:]), COPY)
        nc.vector.tensor_copy(f1[:].indirect(o3[:]), ga[:])
        a6 = keep.tile([P, I], F32, name="a6")
        nc.scalar.activation(a6[:], a[:].indirect(o6[:]), COPY)
        b5 = keep.tile([P, I], F32, name="b5", tag="a")
        nc.scalar.activation(b5[:], b[:].indirect(o5[:]), COPY)

        m1 = keep.tile([P, Z], F32, name="m1")
        nc.vector.tensor_tensor(m1[:], f1[:], f2[:], ALU.min)

        g3 = [keep.tile([P, HALF], F32, name="g3%d" % h) for h in range(2)]
        t4 = [keep.tile([P, HALF], F32, name="t4%d" % h) for h in range(2)]
        v = [keep.tile([P, HALF], F32, name="v%d" % h) for h in range(2)]
        y = [keep.tile([P, HALF], F32, name="y%d" % h) for h in range(2)]
        for h in range(2):
            s = slice(HALF * h, HALF * (h + 1))
            nc.scalar.activation(g3[h][:], m1[:].indirect(o3[:, cols(s.start, s.stop)]), COPY)
            nc.vector.tensor_tensor(t4[h][:], m1[:].indirect(o4[:, cols(s.start, s.stop)]), b5[:, s], ALU.subtract)
        for h in range(2):
            nc.vector.tensor_tensor(v[h][:], t4[h][:], g3[h][:], ALU.add)
        for h in range(2):
            s = slice(HALF * h, HALF * (h + 1))
            nc.vector.tensor_tensor(y[h][:], v[h][:], a6[:, s], ALU.max)
            nc.sync.dma_start(out[:, s], y[h][:])
